import numpy as np
import ml_dtypes


def mxq(x, axis, fmt="e4m3"):
    dtype, down = {"e4m3": (ml_dtypes.float8_e4m3fn, 7), "e5m2": (ml_dtypes.float8_e5m2, 14)}[fmt]
    v = np.moveaxis(np.asarray(x, np.float32).astype(ml_dtypes.bfloat16).astype(np.float64), axis, -1)
    blocks = v.reshape(v.shape[:-1] + (-1, 32))
    amax = np.abs(blocks).max(-1, keepdims=True)
    byte = np.maximum(np.where(amax > 0, np.frexp(amax)[1] - 1 + 127, 0) - down, 1)
    scale = np.exp2(byte - 127.0)
    codes = (blocks / scale).astype(np.float32).astype(dtype).astype(np.float64)
    return np.moveaxis((codes * scale).reshape(v.shape), -1, axis)


WIDE = False


def mx_kscale(k):
    if not WIDE:
        return np.ones(k)
    levels = np.array([10, -10, 5, -5, 0])
    if k % 512:
        return np.exp2(np.random.permutation(np.resize(levels, k // 32))).repeat(32)
    a = np.empty((k // 512, 16))
    for p in range(k // 512):
        a[p, :8] = np.random.permutation(np.resize(levels, 8))
        for g in range(8):
            far = levels[np.abs(levels - a[p, g]) >= 10]
            a[p, g + 8] = far[np.random.randint(len(far))]
    return np.exp2(a.ravel()).repeat(32)


def f64(x):
    return np.asarray(x).astype(np.float64)


def striped(idx):
    return np.tile(idx.reshape(-1, 16).T, (8, 1)).astype(np.uint16)


def unstriped(offs):
    return offs[:16].T.reshape(-1).astype(np.int64)


def striped8(idx):
    return np.concatenate([x.reshape(-1, 16).T for x in idx]).astype(np.uint16)


def runs(offs, k):
    lists = np.stack([offs[16 * r : 16 * r + 16].T.reshape(-1) for r in range(8)]).astype(np.int64)
    return lists[np.arange(k) % 512 // 64]


def pack_weight(w):
    k, n = w.shape
    w = f64(np.asarray(w, np.float32).astype(ml_dtypes.bfloat16)).reshape(k // 32, 32, n)
    amax = np.abs(w).max(1)
    byte = np.clip(np.where(amax > 0, np.frexp(amax)[1] - 1 + 127 - 7, 1), 1, 254)
    scaled = (w * np.exp2(127.0 - byte)[:, None, :]).reshape(k, n).astype(np.float32)
    words = np.ascontiguousarray(scaled.reshape(k // 512, 128, 4, n).transpose(0, 1, 3, 2)).astype(ml_dtypes.float8_e4m3fn).view(np.uint8)
    return words, np.ascontiguousarray(byte.astype(np.uint8).reshape(k // 512, 16, n))


def unpack_weight(words, scales):
    g, p, n, _ = words.shape
    vals = np.ascontiguousarray(words).view(ml_dtypes.float8_e4m3fn).astype(np.float64) * np.repeat(np.exp2(scales.astype(np.float64) - 127.0), 8, axis=1)[..., None]
    return vals.transpose(0, 1, 3, 2).reshape(g * 512, n)

def planes(y):
    n, m = y.shape
    v = y.astype(np.float32).astype(ml_dtypes.bfloat16).astype(np.float64).reshape(n // 32, 32, m)
    top = np.abs(v).max(1)
    byte = np.clip(np.where(top > 0, np.frexp(top)[1] - 1 + 127 - 7, 1), 1, 254)
    codes = (v * np.exp2(127.0 - byte)[:, None, :]).reshape(n, m).astype(np.float32).astype(ml_dtypes.float8_e4m3fn).view(np.uint8)
    words = codes.reshape(n // 512, 128, 4, m).transpose(0, 1, 3, 2)
    return np.ascontiguousarray(words), np.ascontiguousarray(byte.astype(np.uint8).reshape(n // 512, 16, m))


K, T, S, N, H = 512, 2048, 512, 512, 512


def setup_inputs():
    n = np.random.standard_normal
    s = mx_kscale(K)[:, None]
    u = mx_kscale(H)
    packed_xT = pack_weight(n((K, T)) * s)
    packed_w1 = pack_weight(n((K, H)) / np.sqrt(K) / s)
    packed_w2 = pack_weight(n((K, H)) / np.sqrt(K) / s)
    packed_w3 = pack_weight(n((K, H)) / np.sqrt(K) / s)
    packed_w4 = pack_weight(n((H, N)) / np.sqrt(H) / u[:, None])
    return {
        "x_words": packed_xT[0],
        "x_scales": packed_xT[1],
        "w1_words": packed_w1[0],
        "w1_scales": packed_w1[1],
        "w2_words": packed_w2[0],
        "w2_scales": packed_w2[1],
        "w3_words": packed_w3[0],
        "w3_scales": packed_w3[1],
        "gn": (np.random.uniform(0.5, 1.5, (H, 1)) * u[:, None]).astype(np.float32),
        "w4_words": packed_w4[0],
        "w4_scales": packed_w4[1],
        "offs": striped(np.random.permutation(T)[:S]),
        "two": striped(np.random.permutation(T)[:S]),
        "three": striped(np.random.permutation(T)[:S]),
        "n1": striped8(np.stack([np.random.permutation(S) for _ in range(8)])),
        "n2": striped8(np.stack([np.random.permutation(S) for _ in range(8)])),
        "n3": striped8(np.stack([np.random.permutation(S) for _ in range(8)])),
        "n4": striped8(np.stack([np.random.permutation(S) for _ in range(8)])),
        "n5": striped8(np.stack([np.random.permutation(S) for _ in range(8)])),
    }


def reference(x_words, x_scales, w1_words, w1_scales, w2_words, w2_scales, w3_words, w3_scales, gn, w4_words, w4_scales, offs, two, three, n1, n2, n3, n4, n5):
    xq = unpack_weight(x_words, x_scales)[:, unstriped(offs)]
    y = unpack_weight(w1_words, w1_scales).T @ xq
    x_two = unpack_weight(x_words, x_scales)[:, unstriped(two)]
    d = unpack_weight(w2_words, w2_scales).T @ x_two
    m1 = np.maximum(y, d[np.arange(H)[:, None], runs(n2, H)]) - (np.minimum(y[np.arange(H)[:, None], runs(n1, H)], d))
    x_three = unpack_weight(x_words, x_scales)[:, unstriped(three)]
    b = unpack_weight(w3_words, w3_scales).T @ x_three
    z = f64(gn) * (m1 * (np.tanh(b[np.arange(H)[:, None], runs(n3, H)] - (b[np.arange(H)[:, None], runs(n4, H)]))))
    h = unpack_weight(w4_words, w4_scales).T @ mxq(z, 0, "e4m3")
    out_0 = np.maximum(h, h[np.arange(N)[:, None], runs(n5, N)])
    return (out_0,) + planes(out_0)

@@ -1,0 +1,201 @@
+from contextlib import ExitStack
+
+import concourse.mybir as mybir
+from concourse.masks import make_identity
+
+F32 = mybir.dt.float32
+BF16 = mybir.dt.bfloat16
+I32 = mybir.dt.int32
+U32 = mybir.dt.uint32
+U16 = mybir.dt.uint16
+U8 = mybir.dt.uint8
+FP8X4 = mybir.dt.float8_e4m3fn_x4
+ALU = mybir.AluOpType
+ACT = mybir.ActivationFunctionType
+
+P = 128
+PACK = 4
+T = 2048
+S = 512
+CH = 128
+NCH = S // CH
+FLOPS = 4 * 2 * 512 * 512 * 512
+STRETCHES = ((0, 256), (256, 384), (384, 512))
+
+
+def tile_picked_triomaxbjointbbig_none_po_kernel(
+    tc, x_words, x_scales, w1_words, w1_scales, w2_words, w2_scales, w3_words, w3_scales, gn,
+    w4_words, w4_scales, offs, two, three, n1, n2, n3, n4, n5, out_0, out_1, out_2,
+):
+    nc = tc.nc
+    with ExitStack() as ctx:
+        keep = ctx.enter_context(tc.tile_pool(name="keep", bufs=1))
+        acc = ctx.enter_context(tc.psum_pool(name="acc", bufs=4))
+        turn = ctx.enter_context(tc.psum_pool(name="turn", bufs=4))
+
+        def words_view(ap):
+            return ap[0].rearrange("p n t -> p (n t)").bitcast(I32)
+
+        def load_list(ap, name):
+            tile = keep.tile([P, S // 16], U16, name=name)
+            nc.sync.dma_start(tile[:], ap)
+            return tile
+
+        def cut(lst, a, b):
+            return lst[:, a // 16 : b // 16]
+
+        def load_scales(queue, tile, plane, ap):
+            for q in range(4):
+                r = 32 * q + 4 * plane
+                queue.dma_start(tile[r : r + 4, :].bitcast(I32), ap[0, 4 * q : 4 * q + 4, :].bitcast(I32))
+
+        xw = keep.tile([P, T], I32, align_bytes=64)
+        xs = keep.tile([P, T], U8, align_bytes=64)
+        ws_raw = keep.tile([P, S], U8, align_bytes=64)
+        ws4_raw = keep.tile([P, S], U8, align_bytes=64)
+        nc.vector.memset(xs[:].bitcast(I32), 0)
+        nc.vector.memset(ws_raw[:].bitcast(I32), 0)
+        nc.vector.memset(ws4_raw[:].bitcast(I32), 0)
+        w_words = (w3_words, w1_words, w2_words, w4_words)
+        w_raw = [keep.tile([P, S], I32, align_bytes=64, name=f"w_raw{a}") for a in range(4)]
+        gain = keep.tile([P, PACK], F32)
+        l_three = load_list(three, "l_three")
+        nc.sync.dma_start(xw[:], words_view(x_words))
+        l_offs = load_list(offs, "l_offs")
+        l_two = load_list(two, "l_two")
+        load_scales(nc.sync, xs, 0, x_scales)
+        for a, ap in enumerate((w3_scales, w1_scales, w2_scales)):
+            load_scales(nc.sync, ws_raw, a, ap)
+        nc.sync.dma_start(w_raw[0][:], words_view(w_words[0]))
+        nc.sync.dma_start(gain[:], gn.rearrange("(p t) o -> p (t o)", t=PACK))
+        for a in (1, 2):
+            nc.sync.dma_start(w_raw[a][:], words_view(w_words[a]))
+        l_n3 = load_list(n3, "l_n3")
+        l_n4 = load_list(n4, "l_n4")
+        l_n2 = load_list(n2, "l_n2")
+        l_n1 = load_list(n1, "l_n1")
+        l_n5 = load_list(n5, "l_n5")
+        nc.sync.dma_start(w_raw[3][:], words_view(w_words[3]))
+        load_scales(nc.sync, ws4_raw, 0, w4_scales)
+
+        ident = keep.tile([P, P], F32)
+        make_identity(nc, ident[:])
+
+        twice_pos = keep.tile([P, PACK], F32)
+        sgn = keep.tile([P, PACK], F32)
+        neg_sgn = keep.tile([P, PACK], F32)
+        mag = keep.tile([P, PACK], F32)
+        neg_mag = keep.tile([P, PACK], F32)
+        nc.gpsimd.tensor_scalar(twice_pos[:], gain[:], 0.0, 2.0, ALU.is_ge, ALU.mult)
+        nc.gpsimd.tensor_scalar(sgn[:], twice_pos[:], 1.0, -1.0, ALU.mult, ALU.add)
+        nc.gpsimd.tensor_scalar(neg_sgn[:], twice_pos[:], -1.0, 1.0, ALU.mult, ALU.add)
+        nc.gpsimd.tensor_tensor(mag[:], gain[:], sgn[:], ALU.mult)
+        nc.gpsimd.tensor_tensor(neg_mag[:], gain[:], neg_sgn[:], ALU.mult)
+
+        ws = keep.tile([P, S], U8, align_bytes=64)
+        ws4 = keep.tile([P, S], U8, align_bytes=64)
+        planes = (ws[0:P, :], ws[4:P, :], ws[8:P, :], ws4[0:P, :])
+        w = [keep.tile([P, S], I32, align_bytes=64, name=f"w{a}") for a in range(4)]
+
+        def deal(dst, src):
+            nc.vector.tensor_copy(dst[:].rearrange("p (t m) -> p m t", t=PACK), src[:].rearrange("p (m t) -> p m t", t=PACK))
+
+        def rows(name):
+            return [keep.tile([P, S], F32, name=f"{name}{t}") for t in range(PACK)]
+
+        def product(out, a, t, codes, scales):
+            cols = slice(P * t, P * (t + 1))
+            nc.tensor.matmul_mx(out, lhsT=w[a][:, cols].bitcast(FP8X4), lhsT_scale=planes[a][:, cols],
+                                rhs=codes.bitcast(FP8X4), rhs_scale=scales, start=True, stop=True)
+
+        b_pos, b_neg, y_neg, d_pos = rows("b_pos"), rows("b_neg"), rows("y_neg"), rows("d_pos")
+        targets = (((b_pos, sgn), (b_neg, neg_sgn)), ((y_neg, neg_mag),), ((d_pos, mag),))
+        lists = (l_three, l_offs, l_two)
+        codes = [keep.tile([P, S], U32, align_bytes=64, name=f"xg{a}") for a in range(3)]
+        scales = [keep.tile([P, S], U8, align_bytes=64, name=f"xgs{a}") for a in range(3)]
+        for a in range(3):
+            nc.vector.tensor_copy(codes[a][:], xw[:].bitcast(U32).indirect(lists[a][:]))
+        for a in range(3):
+            nc.vector.tensor_copy(scales[a][:], xs[:].indirect(lists[a][:]))
+            if a == 0:
+                deal(ws, ws_raw)
+            deal(w[a], w_raw[a])
+            for t in range(PACK):
+                bank = acc.tile([P, S], F32, tag="acc", name="bank")
+                product(bank[:], a, t, codes[a][:], scales[a][:])
+                for dst, factor in targets[a]:
+                    nc.scalar.activation(dst[t][:], bank[:], ACT.Copy, scale=factor[:, t : t + 1])
+
+        def add_turned(bank, first, second, cols):
+            for t in range(PACK):
+                nc.tensor.matmul(bank[:, t, :], first[t][:, cols], ident[:], start=True, stop=False, is_transpose=True)
+                nc.tensor.matmul(bank[:, t, :], second[t][:, cols], ident[:], start=False, stop=True, is_transpose=True)
+
+        b3, b4 = rows("b3"), rows("b4")
+        gate = [keep.tile([P, 2, P, 2], F32, name=f"gate{c}") for c in range(NCH)]
+        for half in range(2):
+            a, b = 256 * half, 256 * (half + 1)
+            for t in range(PACK):
+                nc.vector.tensor_copy(b3[t][:, a:b], b_pos[t][:].indirect(cut(l_n3, a, b)))
+                nc.vector.tensor_copy(b4[t][:, a:b], b_neg[t][:].indirect(cut(l_n4, a, b)))
+            for c in range(a // CH, b // CH):
+                bank = turn.tile([P, PACK, CH], F32, tag="turn", name="diff")
+                add_turned(bank, b3, b4, slice(CH * c, CH * (c + 1)))
+                nc.scalar.activation(gate[c][:], bank[:].rearrange("n (u e) p -> n u p e", e=2), ACT.Tanh)
+
+        larger, smaller = rows("larger"), rows("smaller")
+        d2 = [keep.tile([P, 256], F32, name=f"d2_{i}") for i in range(2)]
+        y1 = [keep.tile([P, 256], F32, name=f"y1_{i}") for i in range(2)]
+        h = rows("h")
+        h_banks = []
+        for a, b in STRETCHES:
+            for t in range(PACK):
+                d_far, y_far = d2[t % 2][:, 0 : b - a], y1[t % 2][:, 0 : b - a]
+                nc.vector.tensor_copy(d_far, d_pos[t][:].indirect(cut(l_n2, a, b)))
+                nc.vector.tensor_copy(y_far, y_neg[t][:].indirect(cut(l_n1, a, b)))
+                nc.vector.scalar_tensor_tensor(larger[t][:, a:b], y_neg[t][:, a:b], -1.0, d_far, ALU.mult, ALU.max)
+                nc.vector.scalar_tensor_tensor(smaller[t][:, a:b], d_pos[t][:, a:b], -1.0, y_far, ALU.mult, ALU.max)
+            for c in range(a // CH, b // CH):
+                cols = slice(CH * c, CH * (c + 1))
+                spread = turn.tile([P, PACK, CH], F32, tag="turn", name="spread")
+                add_turned(spread, larger, smaller, cols)
+                z_turned = keep.tile([P, 2, P, 2], BF16, align_bytes=64, name=f"z_turned{c}")
+                nc.vector.tensor_tensor(z_turned[:], spread[:].rearrange("n (u e) p -> n u p e", e=2), gate[c][:], ALU.mult)
+                pairs = z_turned[:].rearrange("n u p e -> n (u p e)").bitcast(F32)
+                back = turn.tile([P, PACK, CH], F32, tag="turn", name="back")
+                for u in range(2):
+                    nc.tensor.transpose(back[:, u, :], pairs[:, P * u : P * (u + 1)], ident[:])
+                z = keep.tile([P, CH * PACK], BF16, align_bytes=64, name=f"z{c}")
+                nc.scalar.copy(z[:].bitcast(F32).rearrange("p (n u) -> p n u", u=2), back[:, 0:2, :].rearrange("p u n -> p n u"))
+                z_codes = keep.tile([P, CH], U32, align_bytes=64, name=f"z_codes{c}")
+                z_scales = keep.tile([P, CH], U8, align_bytes=64, name=f"z_scales{c}")
+                nc.vector.quantize_mx(z_codes[:].bitcast(FP8X4), z_scales[:], z[:])
+                if c == 0:
+                    deal(ws4, ws4_raw)
+                    deal(w[3], w_raw[3])
+                bank = acc.tile([P, PACK, CH], F32, tag="acc", name="h_bank")
+                for t in range(PACK):
+                    product(bank[:, t, :], 3, t, z_codes[:], z_scales[:])
+                for t in range(PACK):
+                    nc.scalar.copy(h[t][:, cols], bank[:, t, :])
+                h_banks.append(bank)
+
+        out_rows = out_0.rearrange("(p t) n -> p t n", t=PACK)
+        out_words = words_view(out_1)
+        o_codes = keep.tile([P, S], I32, align_bytes=64)
+        o_scales = keep.tile([P, S], U8, align_bytes=64)
+        for a, b in STRETCHES:
+            h5 = keep.tile([P, PACK, b - a], F32, name=f"h5_{a}")
+            for t in range(PACK):
+                nc.vector.tensor_copy(h5[:, t, :], h[t][:].indirect(cut(l_n5, a, b)))
+            result = keep.tile([P, PACK, b - a], F32, name=f"result{a}")
+            for c in range(a // CH, b // CH):
+                cols = slice(CH * c - a, CH * (c + 1) - a)
+                nc.vector.tensor_tensor(result[:, :, cols], h5[:, :, cols], h_banks[c][:], ALU.max)
+            nc.sync.dma_start(out_rows[:, :, a:b], result[:])
+            rounded = keep.tile([P, b - a, PACK], BF16, align_bytes=64, name=f"rounded{a}")
+            nc.scalar.copy(rounded[:], result[:].rearrange("p t n -> p n t"))
+            nc.vector.quantize_mx(o_codes[:, a:b].bitcast(FP8X4), o_scales[:, a:b], rounded[:].rearrange("p n t -> p (n t)"))
+            nc.sync.dma_start(out_words[:, a:b], o_codes[:, a:b])
+        for q in range(4):
+            nc.scalar.dma_start(out_2[0, 4 * q : 4 * q + 4, :].bitcast(I32), o_scales[32 * q : 32 * q + 4, :].bitcast(I32))

@@ -51,36 +51,42 @@ def tile_picked_triomaxbjointbbig_none_po_kernel(
 
         xw = keep.tile([P, T], I32, align_bytes=64)
         xs = keep.tile([P, T], U8, align_bytes=64)
-        ws_raw = keep.tile([P, S], U8, align_bytes=64)
+        ws12_raw = keep.tile([P, S], U8, align_bytes=64)
+        ws3_raw = keep.tile([P, S], U8, align_bytes=64)
         ws4_raw = keep.tile([P, S], U8, align_bytes=64)
-        nc.vector.memset(xs[:].bitcast(I32), 0)
-        nc.vector.memset(ws_raw[:].bitcast(I32), 0)
-        nc.vector.memset(ws4_raw[:].bitcast(I32), 0)
-        w_words = (w3_words, w1_words, w2_words, w4_words)
+        gain_rows = keep.tile([P, P], F32)
+        nc.gpsimd.memset(gain_rows[:], 0.0)
+        for tile in (ws12_raw, xs, ws3_raw, ws4_raw):
+            nc.gpsimd.memset(tile[:].bitcast(I32), 0)
+        w_words = (w1_words, w2_words, w3_words, w4_words)
         w_raw = [keep.tile([P, S], I32, align_bytes=64, name=f"w_raw{a}") for a in range(4)]
-        gain = keep.tile([P, PACK], F32)
-        l_three = load_list(three, "l_three")
-        nc.sync.dma_start(xw[:], words_view(x_words))
         l_offs = load_list(offs, "l_offs")
+        nc.sync.dma_start(xw[:], words_view(x_words))
         l_two = load_list(two, "l_two")
-        load_scales(nc.sync, xs, 0, x_scales)
-        for a, ap in enumerate((w3_scales, w1_scales, w2_scales)):
-            load_scales(nc.sync, ws_raw, a, ap)
+        l_three = load_list(three, "l_three")
         nc.sync.dma_start(w_raw[0][:], words_view(w_words[0]))
-        nc.sync.dma_start(gain[:], gn.rearrange("(p t) o -> p (t o)", t=PACK))
-        for a in (1, 2):
-            nc.sync.dma_start(w_raw[a][:], words_view(w_words[a]))
-        l_n3 = load_list(n3, "l_n3")
-        l_n4 = load_list(n4, "l_n4")
+        load_scales(nc.scalar, xs, 0, x_scales)
+        nc.scalar.dma_start(gain_rows[0:PACK, :].rearrange("t (g q) -> t g q", q=16), gn.rearrange("(g t q) o -> t g (q o)", t=PACK, q=16))
+        load_scales(nc.scalar, ws12_raw, 0, w1_scales)
+        load_scales(nc.scalar, ws12_raw, 1, w2_scales)
+        nc.sync.dma_start(w_raw[1][:], words_view(w_words[1]))
         l_n2 = load_list(n2, "l_n2")
         l_n1 = load_list(n1, "l_n1")
-        l_n5 = load_list(n5, "l_n5")
+        nc.sync.dma_start(w_raw[2][:], words_view(w_words[2]))
+        load_scales(nc.sync, ws3_raw, 0, w3_scales)
+        l_n3 = load_list(n3, "l_n3")
+        l_n4 = load_list(n4, "l_n4")
         nc.sync.dma_start(w_raw[3][:], words_view(w_words[3]))
         load_scales(nc.sync, ws4_raw, 0, w4_scales)
+        l_n5 = load_list(n5, "l_n5")
 
         ident = keep.tile([P, P], F32)
         make_identity(nc, ident[:])
 
+        gain = keep.tile([P, PACK], F32)
+        gain_bank = turn.tile([P, PACK, CH], F32, tag="turn", name="gain_bank")
+        nc.tensor.transpose(gain_bank[:, 0, :], gain_rows[:], ident[:])
+        nc.scalar.copy(gain[:], gain_bank[:, 0, 0:PACK])
         twice_pos = keep.tile([P, PACK], F32)
         sgn = keep.tile([P, PACK], F32)
         neg_sgn = keep.tile([P, PACK], F32)
@@ -92,13 +98,18 @@ def tile_picked_triomaxbjointbbig_none_po_kernel(
         nc.gpsimd.tensor_tensor(mag[:], gain[:], sgn[:], ALU.mult)
         nc.gpsimd.tensor_tensor(neg_mag[:], gain[:], neg_sgn[:], ALU.mult)
 
-        ws = keep.tile([P, S], U8, align_bytes=64)
+        ws3 = keep.tile([P, S], U8, align_bytes=64)
+        ws12 = keep.tile([P, S], U8, align_bytes=64)
         ws4 = keep.tile([P, S], U8, align_bytes=64)
-        planes = (ws[0:P, :], ws[4:P, :], ws[8:P, :], ws4[0:P, :])
+        planes = (ws12[0:P, :], ws12[4:P, :], ws3[0:P, :], ws4[0:P, :])
         w = [keep.tile([P, S], I32, align_bytes=64, name=f"w{a}") for a in range(4)]
 
         def deal(dst, src):
             nc.vector.tensor_copy(dst[:].rearrange("p (t m) -> p m t", t=PACK), src[:].rearrange("p (m t) -> p m t", t=PACK))
+
+        def deal_runs(dst, src, run):
+            nc.vector.tensor_copy(dst[:].bitcast(I32).rearrange("p (t g q) -> p g t q", t=PACK, q=run),
+                                  src[:].bitcast(I32).rearrange("p (g t q) -> p g t q", t=PACK, q=run))
 
         def rows(name):
             return [keep.tile([P, S], F32, name=f"{name}{t}") for t in range(PACK)]
@@ -108,9 +119,9 @@ def tile_picked_triomaxbjointbbig_none_po_kernel(
             nc.tensor.matmul_mx(out, lhsT=w[a][:, cols].bitcast(FP8X4), lhsT_scale=planes[a][:, cols],
                                 rhs=codes.bitcast(FP8X4), rhs_scale=scales, start=True, stop=True)
 
-        b_pos, b_neg, y_neg, d_pos = rows("b_pos"), rows("b_neg"), rows("y_neg"), rows("d_pos")
-        targets = (((b_pos, sgn), (b_neg, neg_sgn)), ((y_neg, neg_mag),), ((d_pos, mag),))
-        lists = (l_three, l_offs, l_two)
+        b_pos, b_neg, y_pos, d_neg = rows("b_pos"), rows("b_neg"), rows("y_pos"), rows("d_neg")
+        targets = (((y_pos, mag),), ((d_neg, neg_mag),), ((b_pos, sgn), (b_neg, neg_sgn)))
+        lists = (l_offs, l_two, l_three)
         codes = [keep.tile([P, S], U32, align_bytes=64, name=f"xg{a}") for a in range(3)]
         scales = [keep.tile([P, S], U8, align_bytes=64, name=f"xgs{a}") for a in range(3)]
         for a in range(3):
@@ -118,80 +129,120 @@ def tile_picked_triomaxbjointbbig_none_po_kernel(
         for a in range(3):
             nc.vector.tensor_copy(scales[a][:], xs[:].indirect(lists[a][:]))
             if a == 0:
-                deal(ws, ws_raw)
-            deal(w[a], w_raw[a])
+                deal_runs(ws12, ws12_raw, 4)
+            if a == 2:
+                deal_runs(ws3, ws3_raw, 4)
+            deal_runs(w[a], w_raw[a], 16)
             for t in range(PACK):
                 bank = acc.tile([P, S], F32, tag="acc", name="bank")
                 product(bank[:], a, t, codes[a][:], scales[a][:])
                 for dst, factor in targets[a]:
                     nc.scalar.activation(dst[t][:], bank[:], ACT.Copy, scale=factor[:, t : t + 1])
 
-        def add_turned(bank, first, second, cols):
-            for t in range(PACK):
-                nc.tensor.matmul(bank[:, t, :], first[t][:, cols], ident[:], start=True, stop=False, is_transpose=True)
-                nc.tensor.matmul(bank[:, t, :], second[t][:, cols], ident[:], start=False, stop=True, is_transpose=True)
+        def add_turned(bank, terms, start, stop):
+            by_tile = bank[:].rearrange("n (g t q) -> n t g q", t=PACK, q=16)
+            for i, (t, term) in enumerate(terms):
+                nc.tensor.matmul(by_tile[:, t, :, :], term, ident[:], start=(start and i == 0),
+                                 stop=(stop and i == len(terms) - 1), is_transpose=True)
 
-        b3, b4 = rows("b3"), rows("b4")
-        gate = [keep.tile([P, 2, P, 2], F32, name=f"gate{c}") for c in range(NCH)]
-        for half in range(2):
-            a, b = 256 * half, 256 * (half + 1)
-            for t in range(PACK):
-                nc.vector.tensor_copy(b3[t][:, a:b], b_pos[t][:].indirect(cut(l_n3, a, b)))
-                nc.vector.tensor_copy(b4[t][:, a:b], b_neg[t][:].indirect(cut(l_n4, a, b)))
-            for c in range(a // CH, b // CH):
-                bank = turn.tile([P, PACK, CH], F32, tag="turn", name="diff")
-                add_turned(bank, b3, b4, slice(CH * c, CH * (c + 1)))
-                nc.scalar.activation(gate[c][:], bank[:].rearrange("n (u e) p -> n u p e", e=2), ACT.Tanh)
+        def by_pairs(bank):
+            return bank[:].rearrange("n (p u e) -> n u p e", u=2, e=2)
 
-        larger, smaller = rows("larger"), rows("smaller")
-        d2 = [keep.tile([P, 256], F32, name=f"d2_{i}") for i in range(2)]
-        y1 = [keep.tile([P, 256], F32, name=f"y1_{i}") for i in range(2)]
+        chunks = [slice(CH * c, CH * (c + 1)) for c in range(NCH)]
+        spread = [acc.tile([P, S], F32, tag="acc", name=f"spread{c}") for c in range(NCH)]
+        gaps = [keep.tile([P, 2, S], F32, name=f"gaps{t}") for t in range(PACK)]
+        excess = [keep.tile([P, 2, S], F32, name=f"excess{t}") for t in range(PACK)]
+        for t in range(PACK):
+            for a, b in ((0, 256), (256, 512)):
+                nc.vector.tensor_tensor(gaps[t][:, 0, a:b], d_neg[t][:].indirect(cut(l_n2, a, b)), y_pos[t][:, a:b], ALU.add)
+                nc.vector.tensor_tensor(gaps[t][:, 1, a:b], y_pos[t][:].indirect(cut(l_n1, a, b)), d_neg[t][:, a:b], ALU.add)
+            nc.scalar.activation(excess[t][:], gaps[t][:], ACT.Relu, scale=-1.0)
+            for c, cols in enumerate(chunks):
+                terms = (y_pos[t][:, cols], d_neg[t][:, cols], excess[t][:, 0, cols], excess[t][:, 1, cols])
+                add_turned(spread[c], [(t, term) for term in terms], t == 0, t == PACK - 1)
+
+        gate = [keep.tile([P, S], F32, name=f"gate{c}") for c in range(NCH)]
+        flat = [g[:].rearrange("p k n -> p (k n)") for g in gaps]
+        homes = ((flat[0], flat[1]), (flat[2][:, 0:S], gate[0][:]), (gate[1][:], flat[3][:, 0:S]))
+        z = [keep.tile([P, 2 * CH * PACK], BF16, align_bytes=64, name=f"z{i}") for i in range(2)]
         h = rows("h")
         h_banks = []
-        for a, b in STRETCHES:
-            for t in range(PACK):
-                d_far, y_far = d2[t % 2][:, 0 : b - a], y1[t % 2][:, 0 : b - a]
-                nc.vector.tensor_copy(d_far, d_pos[t][:].indirect(cut(l_n2, a, b)))
-                nc.vector.tensor_copy(y_far, y_neg[t][:].indirect(cut(l_n1, a, b)))
-                nc.vector.scalar_tensor_tensor(larger[t][:, a:b], y_neg[t][:, a:b], -1.0, d_far, ALU.mult, ALU.max)
-                nc.vector.scalar_tensor_tensor(smaller[t][:, a:b], d_pos[t][:, a:b], -1.0, y_far, ALU.mult, ALU.max)
-            for c in range(a // CH, b // CH):
-                cols = slice(CH * c, CH * (c + 1))
-                spread = turn.tile([P, PACK, CH], F32, tag="turn", name="spread")
-                add_turned(spread, larger, smaller, cols)
-                z_turned = keep.tile([P, 2, P, 2], BF16, align_bytes=64, name=f"z_turned{c}")
-                nc.vector.tensor_tensor(z_turned[:], spread[:].rearrange("n (u e) p -> n u p e", e=2), gate[c][:], ALU.mult)
-                pairs = z_turned[:].rearrange("n u p e -> n (u p e)").bitcast(F32)
-                back = turn.tile([P, PACK, CH], F32, tag="turn", name="back")
-                for u in range(2):
-                    nc.tensor.transpose(back[:, u, :], pairs[:, P * u : P * (u + 1)], ident[:])
-                z = keep.tile([P, CH * PACK], BF16, align_bytes=64, name=f"z{c}")
-                nc.scalar.copy(z[:].bitcast(F32).rearrange("p (n u) -> p n u", u=2), back[:, 0:2, :].rearrange("p u n -> p n u"))
-                z_codes = keep.tile([P, CH], U32, align_bytes=64, name=f"z_codes{c}")
-                z_scales = keep.tile([P, CH], U8, align_bytes=64, name=f"z_scales{c}")
-                nc.vector.quantize_mx(z_codes[:].bitcast(FP8X4), z_scales[:], z[:])
-                if c == 0:
-                    deal(ws4, ws4_raw)
-                    deal(w[3], w_raw[3])
-                bank = acc.tile([P, PACK, CH], F32, tag="acc", name="h_bank")
-                for t in range(PACK):
-                    product(bank[:, t, :], 3, t, z_codes[:], z_scales[:])
-                for t in range(PACK):
-                    nc.scalar.copy(h[t][:, cols], bank[:, t, :])
+
+        def look_up_b(i, t):
+            a, b = STRETCHES[i]
+            home = homes[i][t // 2].rearrange("p (t k n) -> p t k n", t=2, k=2)
+            nc.vector.tensor_copy(home[:, t % 2, 0, :], b_pos[t][:].indirect(cut(l_n3, a, b)))
+            nc.vector.tensor_copy(home[:, t % 2, 1, :], b_neg[t][:].indirect(cut(l_n4, a, b)))
+
+        def make_gate(i, c, order):
+            a = STRETCHES[i][0]
+            cols = slice(CH * c - a, CH * (c + 1) - a)
+            bank = turn.tile([P, S], F32, tag="turn", name="diff")
+            terms = []
+            for t in order:
+                home = homes[i][t // 2].rearrange("p (t k n) -> p t k n", t=2, k=2)
+                terms.extend([(t, home[:, t % 2, 0, cols]), (t, home[:, t % 2, 1, cols])])
+            add_turned(bank, terms, True, True)
+            nc.scalar.activation(gate[c][:].rearrange("n (u p e) -> n u p e", u=2, e=2), by_pairs(bank), ACT.Tanh)
+
+        def make_z(c):
+            z_turned = keep.tile([P, 2, P, 2], BF16, align_bytes=64, name=f"z_turned{c}")
+            nc.vector.tensor_tensor(z_turned[:], by_pairs(spread[c]), gate[c][:].rearrange("n (u p e) -> n u p e", u=2, e=2), ALU.mult)
+            pairs = z_turned[:].rearrange("n u p e -> n (u p e)").bitcast(F32)
+            back = turn.tile([P, PACK, CH], F32, tag="turn", name="back")
+            for u in range(2):
+                nc.tensor.transpose(back[:, u, :], pairs[:, P * u : P * (u + 1)], ident[:])
+            words = z[c // 2][:].bitcast(F32).rearrange("p (n u) -> p n u", u=2)
+            nc.scalar.copy(words[:, chunks[c % 2], :], back[:, 0:2, :].rearrange("p u n -> p n u"))
+
+        def second_layer(i):
+            z_codes = keep.tile([P, 2 * CH], U32, align_bytes=64, name=f"z_codes{i}")
+            z_scales = keep.tile([P, 2 * CH], U8, align_bytes=64, name=f"z_scales{i}")
+            nc.vector.quantize_mx(z_codes[:].bitcast(FP8X4), z_scales[:], z[i][:])
+            for pair in range(2):
+                bank = acc.tile([P, 2, 2 * CH], F32, tag="acc", name="h_bank")
+                for k in range(2):
+                    product(bank[:, k, :], 3, 2 * pair + k, z_codes[:], z_scales[:])
+                for k in range(2):
+                    nc.scalar.copy(h[2 * pair + k][:, 2 * CH * i : 2 * CH * (i + 1)], bank[:, k, :])
                 h_banks.append(bank)
+
+        for t in range(PACK):
+            look_up_b(0, t)
+        make_gate(0, 0, (0, 1, 2, 3))
+        make_gate(0, 1, (0, 1, 2, 3))
+        deal(ws4, ws4_raw)
+        deal(w[3], w_raw[3])
+        look_up_b(1, 0)
+        look_up_b(1, 1)
+        look_up_b(2, 2)
+        look_up_b(2, 3)
+        make_z(0)
+        look_up_b(1, 2)
+        look_up_b(1, 3)
+        make_gate(1, 2, (0, 1, 2, 3))
+        make_z(1)
+        second_layer(0)
+        look_up_b(2, 0)
+        look_up_b(2, 1)
+        make_gate(2, 3, (2, 3, 0, 1))
+        make_z(2)
+        make_z(3)
+        second_layer(1)
 
         out_rows = out_0.rearrange("(p t) n -> p t n", t=PACK)
         out_words = words_view(out_1)
         o_codes = keep.tile([P, S], I32, align_bytes=64)
         o_scales = keep.tile([P, S], U8, align_bytes=64)
+        h5 = keep.tile([P, PACK, 256], F32)
         for a, b in STRETCHES:
-            h5 = keep.tile([P, PACK, b - a], F32, name=f"h5_{a}")
             for t in range(PACK):
-                nc.vector.tensor_copy(h5[:, t, :], h[t][:].indirect(cut(l_n5, a, b)))
+                nc.vector.tensor_copy(h5[:, t, a % 256 : a % 256 + b - a], h[t][:].indirect(cut(l_n5, a, b)))
             result = keep.tile([P, PACK, b - a], F32, name=f"result{a}")
-            for c in range(a // CH, b // CH):
-                cols = slice(CH * c - a, CH * (c + 1) - a)
-                nc.vector.tensor_tensor(result[:, :, cols], h5[:, :, cols], h_banks[c][:], ALU.max)
+            cols = slice(a % 256, a % 256 + b - a)
+            for pair in range(2):
+                both = slice(2 * pair, 2 * pair + 2)
+                nc.vector.tensor_tensor(result[:, both, :], h5[:, both, cols], h_banks[2 * (a // 256) + pair][:, :, cols], ALU.max)
             nc.sync.dma_start(out_rows[:, :, a:b], result[:])
             rounded = keep.tile([P, b - a, PACK], BF16, align_bytes=64, name=f"rounded{a}")
             nc.scalar.copy(rounded[:], result[:].rearrange("p t n -> p n t"))

@@ -44,64 +44,55 @@ def tile_picked_triomaxbjointbbig_none_po_kernel(
         def cut(lst, a, b):
             return lst[:, a // 16 : b // 16]
 
-        def load_scales(queue, tile, plane, ap):
+        def load_scales(queue, tile, ap):
             for q in range(4):
-                r = 32 * q + 4 * plane
+                r = 32 * q
                 queue.dma_start(tile[r : r + 4, :].bitcast(I32), ap[0, 4 * q : 4 * q + 4, :].bitcast(I32))
 
-        xw = keep.tile([P, T], I32, align_bytes=64)
-        xs = keep.tile([P, T], U8, align_bytes=64)
-        ws12_raw = keep.tile([P, S], U8, align_bytes=64)
-        ws3_raw = keep.tile([P, S], U8, align_bytes=64)
-        ws4_raw = keep.tile([P, S], U8, align_bytes=64)
-        gain_rows = keep.tile([P, P], F32)
+        xw = keep.tile([P, T], I32, align_bytes=64, name="xw")
+        xs = keep.tile([P, T], U8, align_bytes=64, name="xs")
+        ws_raw = [keep.tile([P, S], U8, align_bytes=64, name=f"ws_raw{a}") for a in range(4)]
+        gain_rows = keep.tile([P, P], F32, name="gain_rows")
+        ident = keep.tile([P, P], F32, name="ident")
         nc.gpsimd.memset(gain_rows[:], 0.0)
-        for tile in (ws12_raw, xs, ws3_raw, ws4_raw):
-            nc.gpsimd.memset(tile[:].bitcast(I32), 0)
+        for tile in (xs, *ws_raw):
+            nc.vector.memset(tile[:].bitcast(I32), 0)
+        make_identity(nc, ident[:])
         w_words = (w1_words, w2_words, w3_words, w4_words)
         w_raw = [keep.tile([P, S], I32, align_bytes=64, name=f"w_raw{a}") for a in range(4)]
         l_offs = load_list(offs, "l_offs")
         nc.sync.dma_start(xw[:], words_view(x_words))
         l_two = load_list(two, "l_two")
-        l_three = load_list(three, "l_three")
-        nc.sync.dma_start(w_raw[0][:], words_view(w_words[0]))
-        load_scales(nc.scalar, xs, 0, x_scales)
         nc.scalar.dma_start(gain_rows[0:PACK, :].rearrange("t (g q) -> t g q", q=16), gn.rearrange("(g t q) o -> t g (q o)", t=PACK, q=16))
-        load_scales(nc.scalar, ws12_raw, 0, w1_scales)
-        load_scales(nc.scalar, ws12_raw, 1, w2_scales)
-        nc.sync.dma_start(w_raw[1][:], words_view(w_words[1]))
+        load_scales(nc.scalar, xs, x_scales)
+        load_scales(nc.scalar, ws_raw[0], w1_scales)
+        for a in range(2):
+            nc.sync.dma_start(w_raw[a][:], words_view(w_words[a]))
+        load_scales(nc.sync, ws_raw[1], w2_scales)
+        l_three = load_list(three, "l_three")
+        nc.sync.dma_start(w_raw[2][:], words_view(w_words[2]))
         l_n2 = load_list(n2, "l_n2")
         l_n1 = load_list(n1, "l_n1")
-        nc.sync.dma_start(w_raw[2][:], words_view(w_words[2]))
-        load_scales(nc.sync, ws3_raw, 0, w3_scales)
+        load_scales(nc.scalar, ws_raw[2], w3_scales)
         l_n3 = load_list(n3, "l_n3")
         l_n4 = load_list(n4, "l_n4")
         nc.sync.dma_start(w_raw[3][:], words_view(w_words[3]))
-        load_scales(nc.sync, ws4_raw, 0, w4_scales)
+        load_scales(nc.sync, ws_raw[3], w4_scales)
         l_n5 = load_list(n5, "l_n5")
 
-        ident = keep.tile([P, P], F32)
-        make_identity(nc, ident[:])
-
-        gain = keep.tile([P, PACK], F32)
         gain_bank = turn.tile([P, PACK, CH], F32, tag="turn", name="gain_bank")
         nc.tensor.transpose(gain_bank[:, 0, :], gain_rows[:], ident[:])
-        nc.scalar.copy(gain[:], gain_bank[:, 0, 0:PACK])
-        twice_pos = keep.tile([P, PACK], F32)
+        gain = gain_bank[:, 0, 0:PACK]
         sgn = keep.tile([P, PACK], F32)
         neg_sgn = keep.tile([P, PACK], F32)
         mag = keep.tile([P, PACK], F32)
         neg_mag = keep.tile([P, PACK], F32)
-        nc.gpsimd.tensor_scalar(twice_pos[:], gain[:], 0.0, 2.0, ALU.is_ge, ALU.mult)
-        nc.gpsimd.tensor_scalar(sgn[:], twice_pos[:], 1.0, -1.0, ALU.mult, ALU.add)
-        nc.gpsimd.tensor_scalar(neg_sgn[:], twice_pos[:], -1.0, 1.0, ALU.mult, ALU.add)
-        nc.gpsimd.tensor_tensor(mag[:], gain[:], sgn[:], ALU.mult)
-        nc.gpsimd.tensor_tensor(neg_mag[:], gain[:], neg_sgn[:], ALU.mult)
+        nc.scalar.activation(mag[:], gain, ACT.Abs)
+        nc.scalar.activation(sgn[:], gain, ACT.Sign)
+        nc.scalar.activation(neg_sgn[:], gain, ACT.Sign, scale=-1.0)
+        nc.scalar.activation(neg_mag[:], mag[:], ACT.Copy, scale=-1.0)
 
-        ws3 = keep.tile([P, S], U8, align_bytes=64)
-        ws12 = keep.tile([P, S], U8, align_bytes=64)
-        ws4 = keep.tile([P, S], U8, align_bytes=64)
-        planes = (ws12[0:P, :], ws12[4:P, :], ws3[0:P, :], ws4[0:P, :])
+        planes = [keep.tile([P, S], U8, align_bytes=64, name=f"ws{a}") for a in range(4)]
         w = [keep.tile([P, S], I32, align_bytes=64, name=f"w{a}") for a in range(4)]
 
         def deal(dst, src):
@@ -120,24 +111,30 @@ def tile_picked_triomaxbjointbbig_none_po_kernel(
                                 rhs=codes.bitcast(FP8X4), rhs_scale=scales, start=True, stop=True)
 
         b_pos, b_neg, y_pos, d_neg = rows("b_pos"), rows("b_neg"), rows("y_pos"), rows("d_neg")
-        targets = (((y_pos, mag),), ((d_neg, neg_mag),), ((b_pos, sgn), (b_neg, neg_sgn)))
+        targets = (((y_pos, mag),), ((d_neg, neg_mag),))
         lists = (l_offs, l_two, l_three)
-        codes = [keep.tile([P, S], U32, align_bytes=64, name=f"xg{a}") for a in range(3)]
-        scales = [keep.tile([P, S], U8, align_bytes=64, name=f"xgs{a}") for a in range(3)]
+        codes, scales = [], []
         for a in range(3):
+            codes.append(keep.tile([P, S], U32, align_bytes=64, name=f"xg{a}", tag=f"xg{a}"))
+            scales.append(keep.tile([P, S], U8, align_bytes=64, name=f"xgs{a}"))
             nc.vector.tensor_copy(codes[a][:], xw[:].bitcast(U32).indirect(lists[a][:]))
-        for a in range(3):
             nc.vector.tensor_copy(scales[a][:], xs[:].indirect(lists[a][:]))
-            if a == 0:
-                deal_runs(ws12, ws12_raw, 4)
-            if a == 2:
-                deal_runs(ws3, ws3_raw, 4)
             deal_runs(w[a], w_raw[a], 16)
-            for t in range(PACK):
-                bank = acc.tile([P, S], F32, tag="acc", name="bank")
-                product(bank[:], a, t, codes[a][:], scales[a][:])
-                for dst, factor in targets[a]:
-                    nc.scalar.activation(dst[t][:], bank[:], ACT.Copy, scale=factor[:, t : t + 1])
+            deal_runs(planes[a], ws_raw[a], 4)
+
+        def first_layer(pool, tag, a, t):
+            bank = pool.tile([P, S], F32, tag=tag, name="bank")
+            product(bank[:], a, t, codes[a][:], scales[a][:])
+            for dst, factor in targets[a]:
+                nc.scalar.activation(dst[t][:, 0:S], bank[:], ACT.Copy, scale=factor[:, t : t + 1])
+
+        for t in range(PACK):
+            first_layer(acc, "acc", 0, t)
+            first_layer(acc, "acc", 1, t)
+
+        b_banks = [turn.tile([P, S], F32, tag="turn", name="b_bank") for t in range(PACK)]
+        for t in range(PACK):
+            product(b_banks[t][:], 2, t, codes[2][:], scales[2][:])
 
         def add_turned(bank, terms, start, stop):
             by_tile = bank[:].rearrange("n (g t q) -> n t g q", t=PACK, q=16)
@@ -145,107 +142,147 @@ def tile_picked_triomaxbjointbbig_none_po_kernel(
                 nc.tensor.matmul(by_tile[:, t, :, :], term, ident[:], start=(start and i == 0),
                                  stop=(stop and i == len(terms) - 1), is_transpose=True)
 
-        def by_pairs(bank):
-            return bank[:].rearrange("n (p u e) -> n u p e", u=2, e=2)
-
         chunks = [slice(CH * c, CH * (c + 1)) for c in range(NCH)]
         spread = [acc.tile([P, S], F32, tag="acc", name=f"spread{c}") for c in range(NCH)]
         gaps = [keep.tile([P, 2, S], F32, name=f"gaps{t}") for t in range(PACK)]
-        excess = [keep.tile([P, 2, S], F32, name=f"excess{t}") for t in range(PACK)]
+        for c, cols in enumerate(chunks):
+            add_turned(spread[c], [(t, x[t][:, cols]) for t in range(PACK) for x in (y_pos, d_neg)], True, False)
         for t in range(PACK):
             for a, b in ((0, 256), (256, 512)):
                 nc.vector.tensor_tensor(gaps[t][:, 0, a:b], d_neg[t][:].indirect(cut(l_n2, a, b)), y_pos[t][:, a:b], ALU.add)
                 nc.vector.tensor_tensor(gaps[t][:, 1, a:b], y_pos[t][:].indirect(cut(l_n1, a, b)), d_neg[t][:, a:b], ALU.add)
-            nc.scalar.activation(excess[t][:], gaps[t][:], ACT.Relu, scale=-1.0)
+            for u in ((0, 1), (2,), (), (3,))[t]:
+                nc.scalar.activation(b_pos[u][:], b_banks[u][:], ACT.Copy, scale=sgn[:, u : u + 1])
+                nc.scalar.activation(b_neg[u][:], b_banks[u][:], ACT.Copy, scale=neg_sgn[:, u : u + 1])
+            excess = keep.tile([P, 2, S], F32, align_bytes=64, name=f"excess{t}", tag=("xg2" if t == 0 else f"excess{t}"))
+            nc.scalar.activation(excess[:], gaps[t][:], ACT.Relu, scale=-1.0)
             for c, cols in enumerate(chunks):
-                terms = (y_pos[t][:, cols], d_neg[t][:, cols], excess[t][:, 0, cols], excess[t][:, 1, cols])
-                add_turned(spread[c], [(t, term) for term in terms], t == 0, t == PACK - 1)
+                add_turned(spread[c], [(t, excess[:, k, cols]) for k in range(2)], False, t == PACK - 1)
 
         gate = [keep.tile([P, S], F32, name=f"gate{c}") for c in range(NCH)]
         flat = [g[:].rearrange("p k n -> p (k n)") for g in gaps]
-        homes = ((flat[0], flat[1]), (flat[2][:, 0:S], gate[0][:]), (gate[1][:], flat[3][:, 0:S]))
-        z = [keep.tile([P, 2 * CH * PACK], BF16, align_bytes=64, name=f"z{i}") for i in range(2)]
+        homes = {}
+
+        def settle(i, tiles, ap):
+            view = ap.rearrange("p (t k n) -> p t k n", t=len(tiles), k=2)
+            for j, t in enumerate(tiles):
+                homes[i, t] = view[:, j, :, :]
+
+        settle(0, (0, 1), flat[2])
+        settle(0, (2, 3), flat[3])
+        settle(1, (0, 1), excess[:, 0, :])
+        settle(1, (2, 3), gate[0][:])
+        settle(2, (0,), gate[1][:, 0 : 2 * CH])
+        z_turned = [keep.tile([P, S], BF16, align_bytes=64, name=f"z_turned{c}") for c in range(NCH)]
+        z_codes = keep.tile([P, S], U32, align_bytes=64)
+        z_scales = keep.tile([P, S], U8, align_bytes=64)
+        z = [keep.tile([P, (b - a) * PACK], BF16, align_bytes=64, name=f"z{a}", tag=f"z{a}") for a, b in STRETCHES]
         h = rows("h")
-        h_banks = []
 
         def look_up_b(i, t):
             a, b = STRETCHES[i]
-            home = homes[i][t // 2].rearrange("p (t k n) -> p t k n", t=2, k=2)
-            nc.vector.tensor_copy(home[:, t % 2, 0, :], b_pos[t][:].indirect(cut(l_n3, a, b)))
-            nc.vector.tensor_copy(home[:, t % 2, 1, :], b_neg[t][:].indirect(cut(l_n4, a, b)))
+            nc.vector.tensor_copy(homes[i, t][:, 0, :], b_pos[t][:].indirect(cut(l_n3, a, b)))
+            nc.vector.tensor_copy(homes[i, t][:, 1, :], b_neg[t][:].indirect(cut(l_n4, a, b)))
 
-        def make_gate(i, c, order):
+        def new_bank(name):
+            return turn.tile([P, S], F32, tag="turn", name=name)
+
+        def add_diff(bank, i, c, tiles, start, stop):
             a = STRETCHES[i][0]
             cols = slice(CH * c - a, CH * (c + 1) - a)
-            bank = turn.tile([P, S], F32, tag="turn", name="diff")
-            terms = []
-            for t in order:
-                home = homes[i][t // 2].rearrange("p (t k n) -> p t k n", t=2, k=2)
-                terms.extend([(t, home[:, t % 2, 0, cols]), (t, home[:, t % 2, 1, cols])])
-            add_turned(bank, terms, True, True)
-            nc.scalar.activation(gate[c][:].rearrange("n (u p e) -> n u p e", u=2, e=2), by_pairs(bank), ACT.Tanh)
+            add_turned(bank, [(t, homes[i, t][:, k, cols]) for t in tiles for k in range(2)], start, stop)
 
-        def make_z(c):
-            z_turned = keep.tile([P, 2, P, 2], BF16, align_bytes=64, name=f"z_turned{c}")
-            nc.vector.tensor_tensor(z_turned[:], by_pairs(spread[c]), gate[c][:].rearrange("n (u p e) -> n u p e", u=2, e=2), ALU.mult)
-            pairs = z_turned[:].rearrange("n u p e -> n (u p e)").bitcast(F32)
+        def part(ap, t0, t1):
+            return ap[:].rearrange("n (g f) -> n g f", g=8)[:, :, 16 * t0 : 16 * t1]
+
+        def make_gate(c, bank, t0, t1):
+            nc.scalar.activation(part(gate[c], t0, t1), part(bank, t0, t1), ACT.Tanh)
+
+        def make_z(c, t0, t1):
+            nc.vector.tensor_tensor(part(z_turned[c], t0, t1), part(spread[c], t0, t1), part(gate[c], t0, t1), ALU.mult)
+
+        def turn_back(c):
+            pairs = z_turned[c][:].bitcast(F32).rearrange("n (p u) -> n u p", u=2)
             back = turn.tile([P, PACK, CH], F32, tag="turn", name="back")
             for u in range(2):
-                nc.tensor.transpose(back[:, u, :], pairs[:, P * u : P * (u + 1)], ident[:])
-            words = z[c // 2][:].bitcast(F32).rearrange("p (n u) -> p n u", u=2)
-            nc.scalar.copy(words[:, chunks[c % 2], :], back[:, 0:2, :].rearrange("p u n -> p n u"))
+                nc.tensor.transpose(back[:, u, :], pairs[:, u, :], ident[:])
+            words = z[max(c - 1, 0)][:].bitcast(F32).rearrange("p (n u) -> p n u", u=2)
+            nc.scalar.copy(words[:, chunks[1 if c == 1 else 0], :], back[:, 0:2, :].rearrange("p u n -> p n u"))
 
         def second_layer(i):
-            z_codes = keep.tile([P, 2 * CH], U32, align_bytes=64, name=f"z_codes{i}")
-            z_scales = keep.tile([P, 2 * CH], U8, align_bytes=64, name=f"z_scales{i}")
-            nc.vector.quantize_mx(z_codes[:].bitcast(FP8X4), z_scales[:], z[i][:])
-            for pair in range(2):
-                bank = acc.tile([P, 2, 2 * CH], F32, tag="acc", name="h_bank")
-                for k in range(2):
-                    product(bank[:, k, :], 3, 2 * pair + k, z_codes[:], z_scales[:])
-                for k in range(2):
-                    nc.scalar.copy(h[2 * pair + k][:, 2 * CH * i : 2 * CH * (i + 1)], bank[:, k, :])
-                h_banks.append(bank)
+            a, b = STRETCHES[i]
+            nc.vector.quantize_mx(z_codes[:, a:b].bitcast(FP8X4), z_scales[:, a:b], z[i][:])
+            per_bank = S // (b - a)
+            banks = []
+            for first in range(0, PACK, per_bank):
+                bank = acc.tile([P, per_bank, b - a], F32, tag="acc", name="h_bank")
+                for k in range(per_bank):
+                    product(bank[:, k, :], 3, first + k, z_codes[:, a:b], z_scales[:, a:b])
+                for k in range(per_bank):
+                    nc.scalar.copy(h[first + k][:, a:b], bank[:, k, :])
+                banks.append((slice(first, first + per_bank), bank))
+            h_banks.append(banks)
 
+        h_banks = []
         for t in range(PACK):
             look_up_b(0, t)
-        make_gate(0, 0, (0, 1, 2, 3))
-        make_gate(0, 1, (0, 1, 2, 3))
-        deal(ws4, ws4_raw)
+        for c in range(2):
+            bank = new_bank("diff")
+            add_diff(bank, 0, c, range(PACK), True, True)
+            make_gate(c, bank, 0, PACK)
+        deal(planes[3], ws_raw[3])
         deal(w[3], w_raw[3])
         look_up_b(1, 0)
         look_up_b(1, 1)
-        look_up_b(2, 2)
-        look_up_b(2, 3)
-        make_z(0)
+        diff2 = new_bank("diff2")
+        add_diff(diff2, 1, 2, (0, 1), True, False)
+        for c in range(2):
+            make_z(c, 0, PACK)
+            turn_back(c)
         look_up_b(1, 2)
         look_up_b(1, 3)
-        make_gate(1, 2, (0, 1, 2, 3))
-        make_z(1)
-        second_layer(0)
+        add_diff(diff2, 1, 2, (2, 3), False, True)
+        make_gate(2, diff2, 0, PACK)
+        diff3 = new_bank("diff3")
         look_up_b(2, 0)
+        add_diff(diff3, 2, 3, (0,), True, False)
+        second_layer(0)
+        tail_home = keep.tile([P, 6 * CH], F32, align_bytes=64, tag="z0")
+        settle(2, (1, 2, 3), tail_home[:])
         look_up_b(2, 1)
-        make_gate(2, 3, (2, 3, 0, 1))
-        make_z(2)
-        make_z(3)
+        look_up_b(2, 2)
+        add_diff(diff3, 2, 3, (1, 2), False, True)
+        make_gate(3, diff3, 0, 3)
+        look_up_b(2, 3)
+        last = new_bank("last")
+        add_diff(last, 2, 3, (3,), True, True)
+        make_gate(3, last, 3, PACK)
+        make_z(2, 0, PACK)
+        turn_back(2)
+        make_z(3, 0, 3)
+        make_z(3, 3, PACK)
+        turn_back(3)
         second_layer(1)
+        second_layer(2)
 
         out_rows = out_0.rearrange("(p t) n -> p t n", t=PACK)
         out_words = words_view(out_1)
         o_codes = keep.tile([P, S], I32, align_bytes=64)
         o_scales = keep.tile([P, S], U8, align_bytes=64)
         h5 = keep.tile([P, PACK, 256], F32)
-        for a, b in STRETCHES:
+        for i, (a, b) in enumerate(STRETCHES):
             for t in range(PACK):
                 nc.vector.tensor_copy(h5[:, t, a % 256 : a % 256 + b - a], h[t][:].indirect(cut(l_n5, a, b)))
             result = keep.tile([P, PACK, b - a], F32, name=f"result{a}")
             cols = slice(a % 256, a % 256 + b - a)
-            for pair in range(2):
-                both = slice(2 * pair, 2 * pair + 2)
-                nc.vector.tensor_tensor(result[:, both, :], h5[:, both, cols], h_banks[2 * (a // 256) + pair][:, :, cols], ALU.max)
+            for tiles, bank in h_banks[i]:
+                nc.vector.tensor_tensor(result[:, tiles, :], h5[:, tiles, cols], bank[:], ALU.max)
             nc.sync.dma_start(out_rows[:, :, a:b], result[:])
             rounded = keep.tile([P, b - a, PACK], BF16, align_bytes=64, name=f"rounded{a}")
-            nc.scalar.copy(rounded[:], result[:].rearrange("p t n -> p n t"))
+            if b == S:
+                nc.vector.tensor_copy(rounded[:], result[:].rearrange("p t n -> p n t"))
+            else:
+                nc.scalar.copy(rounded[:], result[:].rearrange("p t n -> p n t"))
             nc.vector.quantize_mx(o_codes[:, a:b].bitcast(FP8X4), o_scales[:, a:b], rounded[:].rearrange("p n t -> p (n t)"))
             nc.sync.dma_start(out_words[:, a:b], o_codes[:, a:b])
         for q in range(4):

@@ -44,43 +44,46 @@ def tile_picked_triomaxbjointbbig_none_po_kernel(
         def cut(lst, a, b):
             return lst[:, a // 16 : b // 16]
 
-        def load_scales(queue, tile, ap):
-            for q in range(4):
-                r = 32 * q
-                queue.dma_start(tile[r : r + 4, :].bitcast(I32), ap[0, 4 * q : 4 * q + 4, :].bitcast(I32))
+        def load_scales(queue, tile, ap, q):
+            queue.dma_start(tile[32 * q : 32 * q + 4, :].bitcast(I32), ap[0, 4 * q : 4 * q + 4, :].bitcast(I32))
 
         xw = keep.tile([P, T], I32, align_bytes=64, name="xw")
         xs = keep.tile([P, T], U8, align_bytes=64, name="xs")
-        ws_raw = [keep.tile([P, S], U8, align_bytes=64, name=f"ws_raw{a}") for a in range(4)]
-        gain_rows = keep.tile([P, P], F32, name="gain_rows")
+        gain_rows = keep.tile([P, P], F32, align_bytes=64, name="gain_rows", tag="early")
         ident = keep.tile([P, P], F32, name="ident")
-        nc.gpsimd.memset(gain_rows[:], 0.0)
-        for tile in (xs, *ws_raw):
-            nc.vector.memset(tile[:].bitcast(I32), 0)
+        ws_all = keep.tile([P, 4 * S], U8, align_bytes=64, name="ws_all")
+        ws_raw = [ws_all[:, S * a : S * (a + 1)] for a in range(4)]
+        nc.gpsimd.memset(xs[:].bitcast(I32), 0)
+        nc.vector.memset(gain_rows[:], 0.0)
+        nc.gpsimd.memset(ws_all[:].bitcast(I32), 0)
         make_identity(nc, ident[:])
         w_words = (w1_words, w2_words, w3_words, w4_words)
-        w_raw = [keep.tile([P, S], I32, align_bytes=64, name=f"w_raw{a}") for a in range(4)]
+        w_raw = [keep.tile([P, S], I32, align_bytes=64, name=f"w_raw{a}", tag=f"w_raw{a}") for a in range(4)]
         l_offs = load_list(offs, "l_offs")
-        nc.sync.dma_start(xw[:], words_view(x_words))
         l_two = load_list(two, "l_two")
-        nc.scalar.dma_start(gain_rows[0:PACK, :].rearrange("t (g q) -> t g q", q=16), gn.rearrange("(g t q) o -> t g (q o)", t=PACK, q=16))
-        load_scales(nc.scalar, xs, x_scales)
-        load_scales(nc.scalar, ws_raw[0], w1_scales)
+        for q in range(4):
+            load_scales(nc.sync if q < 2 else nc.scalar, xs, x_scales, q)
+        nc.sync.dma_start(xw[:], words_view(x_words))
+        nc.sync.dma_start(gain_rows[0:PACK, :].rearrange("t (g q) -> t g q", q=16), gn.rearrange("(g t q) o -> t g (q o)", t=PACK, q=16))
+        for q in range(4):
+            load_scales(nc.scalar, ws_raw[0], w1_scales, q)
+            load_scales(nc.scalar, ws_raw[1], w2_scales, q)
         for a in range(2):
             nc.sync.dma_start(w_raw[a][:], words_view(w_words[a]))
-        load_scales(nc.sync, ws_raw[1], w2_scales)
-        l_three = load_list(three, "l_three")
-        nc.sync.dma_start(w_raw[2][:], words_view(w_words[2]))
         l_n2 = load_list(n2, "l_n2")
         l_n1 = load_list(n1, "l_n1")
-        load_scales(nc.scalar, ws_raw[2], w3_scales)
+        l_three = load_list(three, "l_three")
+        nc.sync.dma_start(w_raw[2][:], words_view(w_words[2]))
+        for q in range(4):
+            load_scales(nc.sync, ws_raw[2], w3_scales, q)
         l_n3 = load_list(n3, "l_n3")
         l_n4 = load_list(n4, "l_n4")
         nc.sync.dma_start(w_raw[3][:], words_view(w_words[3]))
-        load_scales(nc.sync, ws_raw[3], w4_scales)
+        for q in range(4):
+            load_scales(nc.sync, ws_raw[3], w4_scales, q)
         l_n5 = load_list(n5, "l_n5")
 
-        gain_bank = turn.tile([P, PACK, CH], F32, tag="turn", name="gain_bank")
+        gain_bank = acc.tile([P, PACK, CH], F32, tag="acc", name="gain_bank")
         nc.tensor.transpose(gain_bank[:, 0, :], gain_rows[:], ident[:])
         gain = gain_bank[:, 0, 0:PACK]
         sgn = keep.tile([P, PACK], F32)
@@ -93,7 +96,8 @@ def tile_picked_triomaxbjointbbig_none_po_kernel(
         nc.scalar.activation(neg_mag[:], mag[:], ACT.Copy, scale=-1.0)
 
         planes = [keep.tile([P, S], U8, align_bytes=64, name=f"ws{a}") for a in range(4)]
-        w = [keep.tile([P, S], I32, align_bytes=64, name=f"w{a}") for a in range(4)]
+        w12 = keep.tile([P, 2 * S], I32, align_bytes=64, name="w12", tag="early")
+        w = [w12[:, 0:S], w12[:, S : 2 * S]] + [keep.tile([P, S], I32, align_bytes=64, name=f"w{a}") for a in (2, 3)]
 
         def deal(dst, src):
             nc.vector.tensor_copy(dst[:].rearrange("p (t m) -> p m t", t=PACK), src[:].rearrange("p (m t) -> p m t", t=PACK))
@@ -115,8 +119,8 @@ def tile_picked_triomaxbjointbbig_none_po_kernel(
         lists = (l_offs, l_two, l_three)
         codes, scales = [], []
         for a in range(3):
-            codes.append(keep.tile([P, S], U32, align_bytes=64, name=f"xg{a}", tag=f"xg{a}"))
-            scales.append(keep.tile([P, S], U8, align_bytes=64, name=f"xgs{a}"))
+            codes.append(keep.tile([P, S], U32, align_bytes=64, name=f"xg{a}", tag=("w_raw0" if a == 2 else f"xg{a}")))
+            scales.append(keep.tile([P, S], U8, align_bytes=64, name=f"xgs{a}", tag=("w_raw1" if a == 2 else f"xgs{a}")))
             nc.vector.tensor_copy(codes[a][:], xw[:].bitcast(U32).indirect(lists[a][:]))
             nc.vector.tensor_copy(scales[a][:], xs[:].indirect(lists[a][:]))
             deal_runs(w[a], w_raw[a], 16)
@@ -129,12 +133,17 @@ def tile_picked_triomaxbjointbbig_none_po_kernel(
                 nc.scalar.activation(dst[t][:, 0:S], bank[:], ACT.Copy, scale=factor[:, t : t + 1])
 
         for t in range(PACK):
-            first_layer(acc, "acc", 0, t)
-            first_layer(acc, "acc", 1, t)
+            for a in range(2):
+                pool, tag = (turn, "turn") if 3 <= 2 * t + a < 7 else (acc, "acc")
+                first_layer(pool, tag, a, t)
 
         b_banks = [turn.tile([P, S], F32, tag="turn", name="b_bank") for t in range(PACK)]
         for t in range(PACK):
             product(b_banks[t][:], 2, t, codes[2][:], scales[2][:])
+
+        def copy_b(t):
+            nc.scalar.activation(b_pos[t][:], b_banks[t][:], ACT.Copy, scale=sgn[:, t : t + 1])
+            nc.scalar.activation(b_neg[t][:], b_banks[t][:], ACT.Copy, scale=neg_sgn[:, t : t + 1])
 
         def add_turned(bank, terms, start, stop):
             by_tile = bank[:].rearrange("n (g t q) -> n t g q", t=PACK, q=16)
@@ -151,10 +160,9 @@ def tile_picked_triomaxbjointbbig_none_po_kernel(
             for a, b in ((0, 256), (256, 512)):
                 nc.vector.tensor_tensor(gaps[t][:, 0, a:b], d_neg[t][:].indirect(cut(l_n2, a, b)), y_pos[t][:, a:b], ALU.add)
                 nc.vector.tensor_tensor(gaps[t][:, 1, a:b], y_pos[t][:].indirect(cut(l_n1, a, b)), d_neg[t][:, a:b], ALU.add)
-            for u in ((0, 1), (2,), (), (3,))[t]:
-                nc.scalar.activation(b_pos[u][:], b_banks[u][:], ACT.Copy, scale=sgn[:, u : u + 1])
-                nc.scalar.activation(b_neg[u][:], b_banks[u][:], ACT.Copy, scale=neg_sgn[:, u : u + 1])
-            excess = keep.tile([P, 2, S], F32, align_bytes=64, name=f"excess{t}", tag=("xg2" if t == 0 else f"excess{t}"))
+            for u in ((0, 1), (), (), (2, 3))[t]:
+                copy_b(u)
+            excess = keep.tile([P, 2, S], F32, align_bytes=64, name=f"excess{t}")
             nc.scalar.activation(excess[:], gaps[t][:], ACT.Relu, scale=-1.0)
             for c, cols in enumerate(chunks):
                 add_turned(spread[c], [(t, excess[:, k, cols]) for k in range(2)], False, t == PACK - 1)
@@ -284,6 +292,8 @@ def tile_picked_triomaxbjointbbig_none_po_kernel(
             else:
                 nc.scalar.copy(rounded[:], result[:].rearrange("p t n -> p n t"))
             nc.vector.quantize_mx(o_codes[:, a:b].bitcast(FP8X4), o_scales[:, a:b], rounded[:].rearrange("p n t -> p (n t)"))
-            nc.sync.dma_start(out_words[:, a:b], o_codes[:, a:b])
+            if i > 0:
+                done = (0, 0, a)[i]
+                nc.sync.dma_start(out_words[:, done:b], o_codes[:, done:b])
         for q in range(4):
-            nc.scalar.dma_start(out_2[0, 4 * q : 4 * q + 4, :].bitcast(I32), o_scales[32 * q : 32 * q + 4, :].bitcast(I32))
+            (nc.scalar, nc.sync)[q % 2].dma_start(out_2[0, 4 * q : 4 * q + 4, :].bitcast(I32), o_scales[32 * q : 32 * q + 4, :].bitcast(I32))

from contextlib import ExitStack

import concourse.mybir as mybir
from concourse.masks import make_identity

F32 = mybir.dt.float32
BF16 = mybir.dt.bfloat16
I32 = mybir.dt.int32
U32 = mybir.dt.uint32
U16 = mybir.dt.uint16
U8 = mybir.dt.uint8
FP8X4 = mybir.dt.float8_e4m3fn_x4
ALU = mybir.AluOpType
ACT = mybir.ActivationFunctionType

P = 128
PACK = 4
T = 2048
S = 512
CH = 128
NCH = S // CH
FLOPS = 4 * 2 * 512 * 512 * 512
STRETCHES = ((0, 256), (256, 384), (384, 512))


def tile_picked_triomaxbjointbbig_none_po_kernel(
    tc, x_words, x_scales, w1_words, w1_scales, w2_words, w2_scales, w3_words, w3_scales, gn,
    w4_words, w4_scales, offs, two, three, n1, n2, n3, n4, n5, out_0, out_1, out_2,
):
    nc = tc.nc
    with ExitStack() as ctx:
        keep = ctx.enter_context(tc.tile_pool(name="keep", bufs=1))
        acc = ctx.enter_context(tc.psum_pool(name="acc", bufs=4))
        turn = ctx.enter_context(tc.psum_pool(name="turn", bufs=4))

        def words_view(ap):
            return ap[0].rearrange("p n t -> p (n t)").bitcast(I32)

        def load_list(ap, name):
            tile = keep.tile([P, S // 16], U16, name=name)
            nc.sync.dma_start(tile[:], ap)
            return tile

        def cut(lst, a, b):
            return lst[:, a // 16 : b // 16]

        def load_scales(queue, tile, ap, q):
            queue.dma_start(tile[32 * q : 32 * q + 4, :].bitcast(I32), ap[0, 4 * q : 4 * q + 4, :].bitcast(I32))

        xw = keep.tile([P, T], I32, align_bytes=64, name="xw")
        xs = keep.tile([P, T], U8, align_bytes=64, name="xs")
        gain_rows = keep.tile([P, P], F32, align_bytes=64, name="gain_rows", tag="early")
        ident = keep.tile([P, P], F32, name="ident")
        ws_all = keep.tile([P, 4 * S], U8, align_bytes=64, name="ws_all")
        ws_raw = [ws_all[:, S * a : S * (a + 1)] for a in range(4)]
        nc.gpsimd.memset(xs[:].bitcast(I32), 0)
        nc.vector.memset(gain_rows[:], 0.0)
        nc.gpsimd.memset(ws_all[:].bitcast(I32), 0)
        make_identity(nc, ident[:])
        w_words = (w1_words, w2_words, w3_words, w4_words)
        w_raw = [keep.tile([P, S], I32, align_bytes=64, name=f"w_raw{a}", tag=f"w_raw{a}") for a in range(4)]
        l_offs = load_list(offs, "l_offs")
        l_two = load_list(two, "l_two")
        for q in range(4):
            load_scales(nc.sync if q < 2 else nc.scalar, xs, x_scales, q)
        nc.sync.dma_start(xw[:], words_view(x_words))
        nc.sync.dma_start(gain_rows[0:PACK, :].rearrange("t (g q) -> t g q", q=16), gn.rearrange("(g t q) o -> t g (q o)", t=PACK, q=16))
        for q in range(4):
            load_scales(nc.scalar, ws_raw[0], w1_scales, q)
            load_scales(nc.scalar, ws_raw[1], w2_scales, q)
        for a in range(2):
            nc.sync.dma_start(w_raw[a][:], words_view(w_words[a]))
        l_n2 = load_list(n2, "l_n2")
        l_n1 = load_list(n1, "l_n1")
        l_three = load_list(three, "l_three")
        nc.sync.dma_start(w_raw[2][:], words_view(w_words[2]))
        for q in range(4):
            load_scales(nc.sync, ws_raw[2], w3_scales, q)
        l_n3 = load_list(n3, "l_n3")
        l_n4 = load_list(n4, "l_n4")
        nc.sync.dma_start(w_raw[3][:], words_view(w_words[3]))
        for q in range(4):
            load_scales(nc.sync, ws_raw[3], w4_scales, q)
        l_n5 = load_list(n5, "l_n5")

        gain_bank = acc.tile([P, PACK, CH], F32, tag="acc", name="gain_bank")
        nc.tensor.transpose(gain_bank[:, 0, :], gain_rows[:], ident[:])
        gain = gain_bank[:, 0, 0:PACK]
        sgn = keep.tile([P, PACK], F32)
        neg_sgn = keep.tile([P, PACK], F32)
        mag = keep.tile([P, PACK], F32)
        neg_mag = keep.tile([P, PACK], F32)
        nc.scalar.activation(mag[:], gain, ACT.Abs)
        nc.scalar.activation(sgn[:], gain, ACT.Sign)
        nc.scalar.activation(neg_sgn[:], gain, ACT.Sign, scale=-1.0)
        nc.scalar.activation(neg_mag[:], mag[:], ACT.Copy, scale=-1.0)

        planes = [keep.tile([P, S], U8, align_bytes=64, name=f"ws{a}") for a in range(4)]
        w12 = keep.tile([P, 2 * S], I32, align_bytes=64, name="w12", tag="early")
        w = [w12[:, 0:S], w12[:, S : 2 * S]] + [keep.tile([P, S], I32, align_bytes=64, name=f"w{a}") for a in (2, 3)]

        def deal(dst, src):
            nc.vector.tensor_copy(dst[:].rearrange("p (t m) -> p m t", t=PACK), src[:].rearrange("p (m t) -> p m t", t=PACK))

        def deal_runs(dst, src, run):
            nc.vector.tensor_copy(dst[:].bitcast(I32).rearrange("p (t g q) -> p g t q", t=PACK, q=run),
                                  src[:].bitcast(I32).rearrange("p (g t q) -> p g t q", t=PACK, q=run))

        def rows(name):
            return [keep.tile([P, S], F32, name=f"{name}{t}") for t in range(PACK)]

        def product(out, a, t, codes, scales):
            cols = slice(P * t, P * (t + 1))
            nc.tensor.matmul_mx(out, lhsT=w[a][:, cols].bitcast(FP8X4), lhsT_scale=planes[a][:, cols],
                                rhs=codes.bitcast(FP8X4), rhs_scale=scales, start=True, stop=True)

        b_pos, b_neg, y_pos, d_neg = rows("b_pos"), rows("b_neg"), rows("y_pos"), rows("d_neg")
        targets = (((y_pos, mag),), ((d_neg, neg_mag),))
        lists = (l_offs, l_two, l_three)
        codes, scales = [], []
        for a in range(3):
            codes.append(keep.tile([P, S], U32, align_bytes=64, name=f"xg{a}", tag=("w_raw0" if a == 2 else f"xg{a}")))
            scales.append(keep.tile([P, S], U8, align_bytes=64, name=f"xgs{a}", tag=("w_raw1" if a == 2 else f"xgs{a}")))
            nc.vector.tensor_copy(codes[a][:], xw[:].bitcast(U32).indirect(lists[a][:]))
            nc.vector.tensor_copy(scales[a][:], xs[:].indirect(lists[a][:]))
            deal_runs(w[a], w_raw[a], 16)
            deal_runs(planes[a], ws_raw[a], 4)

        def first_layer(pool, tag, a, t):
            bank = pool.tile([P, S], F32, tag=tag, name="bank")
            product(bank[:], a, t, codes[a][:], scales[a][:])
            for dst, factor in targets[a]:
                nc.scalar.activation(dst[t][:, 0:S], bank[:], ACT.Copy, scale=factor[:, t : t + 1])

        for t in range(PACK):
            for a in range(2):
                pool, tag = (turn, "turn") if 3 <= 2 * t + a < 7 else (acc, "acc")
                first_layer(pool, tag, a, t)

        b_banks = [turn.tile([P, S], F32, tag="turn", name="b_bank") for t in range(PACK)]
        for t in range(PACK):
            product(b_banks[t][:], 2, t, codes[2][:], scales[2][:])

        def copy_b(t):
            nc.scalar.activation(b_pos[t][:], b_banks[t][:], ACT.Copy, scale=sgn[:, t : t + 1])
            nc.scalar.activation(b_neg[t][:], b_banks[t][:], ACT.Copy, scale=neg_sgn[:, t : t + 1])

        def add_turned(bank, terms, start, stop):
            by_tile = bank[:].rearrange("n (g t q) -> n t g q", t=PACK, q=16)
            for i, (t, term) in enumerate(terms):
                nc.tensor.matmul(by_tile[:, t, :, :], term, ident[:], start=(start and i == 0),
                                 stop=(stop and i == len(terms) - 1), is_transpose=True)

        chunks = [slice(CH * c, CH * (c + 1)) for c in range(NCH)]
        spread = [acc.tile([P, S], F32, tag="acc", name=f"spread{c}") for c in range(NCH)]
        gaps = [keep.tile([P, 2, S], F32, name=f"gaps{t}") for t in range(PACK)]
        for c, cols in enumerate(chunks):
            add_turned(spread[c], [(t, x[t][:, cols]) for t in range(PACK) for x in (y_pos, d_neg)], True, False)
        for t in range(PACK):
            for a, b in ((0, 256), (256, 512)):
                nc.vector.tensor_tensor(gaps[t][:, 0, a:b], d_neg[t][:].indirect(cut(l_n2, a, b)), y_pos[t][:, a:b], ALU.add)
                nc.vector.tensor_tensor(gaps[t][:, 1, a:b], y_pos[t][:].indirect(cut(l_n1, a, b)), d_neg[t][:, a:b], ALU.add)
            for u in ((0, 1), (), (), (2, 3))[t]:
                copy_b(u)
            excess = keep.tile([P, 2, S], F32, align_bytes=64, name=f"excess{t}")
            nc.scalar.activation(excess[:], gaps[t][:], ACT.Relu, scale=-1.0)
            for c, cols in enumerate(chunks):
                add_turned(spread[c], [(t, excess[:, k, cols]) for k in range(2)], False, t == PACK - 1)

        gate = [keep.tile([P, S], F32, name=f"gate{c}") for c in range(NCH)]
        flat = [g[:].rearrange("p k n -> p (k n)") for g in gaps]
        homes = {}

        def settle(i, tiles, ap):
            view = ap.rearrange("p (t k n) -> p t k n", t=len(tiles), k=2)
            for j, t in enumerate(tiles):
                homes[i, t] = view[:, j, :, :]

        settle(0, (0, 1), flat[2])
        settle(0, (2, 3), flat[3])
        settle(1, (0, 1), excess[:, 0, :])
        settle(1, (2, 3), gate[0][:])
        settle(2, (0,), gate[1][:, 0 : 2 * CH])
        z_turned = [keep.tile([P, S], BF16, align_bytes=64, name=f"z_turned{c}") for c in range(NCH)]
        z_codes = keep.tile([P, S], U32, align_bytes=64)
        z_scales = keep.tile([P, S], U8, align_bytes=64)
        z = [keep.tile([P, (b - a) * PACK], BF16, align_bytes=64, name=f"z{a}", tag=f"z{a}") for a, b in STRETCHES]
        h = rows("h")

        def look_up_b(i, t):
            a, b = STRETCHES[i]
            nc.vector.tensor_copy(homes[i, t][:, 0, :], b_pos[t][:].indirect(cut(l_n3, a, b)))
            nc.vector.tensor_copy(homes[i, t][:, 1, :], b_neg[t][:].indirect(cut(l_n4, a, b)))

        def new_bank(name):
            return turn.tile([P, S], F32, tag="turn", name=name)

        def add_diff(bank, i, c, tiles, start, stop):
            a = STRETCHES[i][0]
            cols = slice(CH * c - a, CH * (c + 1) - a)
            add_turned(bank, [(t, homes[i, t][:, k, cols]) for t in tiles for k in range(2)], start, stop)

        def part(ap, t0, t1):
            return ap[:].rearrange("n (g f) -> n g f", g=8)[:, :, 16 * t0 : 16 * t1]

        def make_gate(c, bank, t0, t1):
            nc.scalar.activation(part(gate[c], t0, t1), part(bank, t0, t1), ACT.Tanh)

        def make_z(c, t0, t1):
            nc.vector.tensor_tensor(part(z_turned[c], t0, t1), part(spread[c], t0, t1), part(gate[c], t0, t1), ALU.mult)

        def turn_back(c):
            pairs = z_turned[c][:].bitcast(F32).rearrange("n (p u) -> n u p", u=2)
            back = turn.tile([P, PACK, CH], F32, tag="turn", name="back")
            for u in range(2):
                nc.tensor.transpose(back[:, u, :], pairs[:, u, :], ident[:])
            words = z[max(c - 1, 0)][:].bitcast(F32).rearrange("p (n u) -> p n u", u=2)
            nc.scalar.copy(words[:, chunks[1 if c == 1 else 0], :], back[:, 0:2, :].rearrange("p u n -> p n u"))

        def second_layer(i):
            a, b = STRETCHES[i]
            nc.vector.quantize_mx(z_codes[:, a:b].bitcast(FP8X4), z_scales[:, a:b], z[i][:])
            per_bank = S // (b - a)
            banks = []
            for first in range(0, PACK, per_bank):
                bank = acc.tile([P, per_bank, b - a], F32, tag="acc", name="h_bank")
                for k in range(per_bank):
                    product(bank[:, k, :], 3, first + k, z_codes[:, a:b], z_scales[:, a:b])
                for k in range(per_bank):
                    nc.scalar.copy(h[first + k][:, a:b], bank[:, k, :])
                banks.append((slice(first, first + per_bank), bank))
            h_banks.append(banks)

        h_banks = []
        for t in range(PACK):
            look_up_b(0, t)
        for c in range(2):
            bank = new_bank("diff")
            add_diff(bank, 0, c, range(PACK), True, True)
            make_gate(c, bank, 0, PACK)
        deal(planes[3], ws_raw[3])
        deal(w[3], w_raw[3])
        look_up_b(1, 0)
        look_up_b(1, 1)
        diff2 = new_bank("diff2")
        add_diff(diff2, 1, 2, (0, 1), True, False)
        for c in range(2):
            make_z(c, 0, PACK)
            turn_back(c)
        look_up_b(1, 2)
        look_up_b(1, 3)
        add_diff(diff2, 1, 2, (2, 3), False, True)
        make_gate(2, diff2, 0, PACK)
        diff3 = new_bank("diff3")
        look_up_b(2, 0)
        add_diff(diff3, 2, 3, (0,), True, False)
        second_layer(0)
        tail_home = keep.tile([P, 6 * CH], F32, align_bytes=64, tag="z0")
        settle(2, (1, 2, 3), tail_home[:])
        look_up_b(2, 1)
        look_up_b(2, 2)
        add_diff(diff3, 2, 3, (1, 2), False, True)
        make_gate(3, diff3, 0, 3)
        look_up_b(2, 3)
        last = new_bank("last")
        add_diff(last, 2, 3, (3,), True, True)
        make_gate(3, last, 3, PACK)
        make_z(2, 0, PACK)
        turn_back(2)
        make_z(3, 0, 3)
        make_z(3, 3, PACK)
        turn_back(3)
        second_layer(1)
        second_layer(2)

        out_rows = out_0.rearrange("(p t) n -> p t n", t=PACK)
        out_words = words_view(out_1)
        o_codes = keep.tile([P, S], I32, align_bytes=64)
        o_scales = keep.tile([P, S], U8, align_bytes=64)
        h5 = keep.tile([P, PACK, 256], F32)
        for i, (a, b) in enumerate(STRETCHES):
            for t in range(PACK):
                nc.vector.tensor_copy(h5[:, t, a % 256 : a % 256 + b - a], h[t][:].indirect(cut(l_n5, a, b)))
            result = keep.tile([P, PACK, b - a], F32, name=f"result{a}")
            cols = slice(a % 256, a % 256 + b - a)
            for tiles, bank in h_banks[i]:
                nc.vector.tensor_tensor(result[:, tiles, :], h5[:, tiles, cols], bank[:], ALU.max)
            nc.sync.dma_start(out_rows[:, :, a:b], result[:])
            rounded = keep.tile([P, b - a, PACK], BF16, align_bytes=64, name=f"rounded{a}")
            if b == S:
                nc.vector.tensor_copy(rounded[:], result[:].rearrange("p t n -> p n t"))
            else:
                nc.scalar.copy(rounded[:], result[:].rearrange("p t n -> p n t"))
            nc.vector.quantize_mx(o_codes[:, a:b].bitcast(FP8X4), o_scales[:, a:b], rounded[:].rearrange("p n t -> p (n t)"))
            if i > 0:
                done = (0, 0, a)[i]
                nc.sync.dma_start(out_words[:, done:b], o_codes[:, done:b])
        for q in range(4):
            (nc.scalar, nc.sync)[q % 2].dma_start(out_2[0, 4 * q : 4 * q + 4, :].bitcast(I32), o_scales[32 * q : 32 * q + 4, :].bitcast(I32))
